import numpy as np
import ml_dtypes


def mxq(x, axis, fmt="e4m3"):
    dtype, down = {"e4m3": (ml_dtypes.float8_e4m3fn, 7), "e5m2": (ml_dtypes.float8_e5m2, 14)}[fmt]
    v = np.moveaxis(np.asarray(x, np.float32).astype(ml_dtypes.bfloat16).astype(np.float64), axis, -1)
    blocks = v.reshape(v.shape[:-1] + (-1, 32))
    amax = np.abs(blocks).max(-1, keepdims=True)
    byte = np.maximum(np.where(amax > 0, np.frexp(amax)[1] - 1 + 127, 0) - down, 1)
    scale = np.exp2(byte - 127.0)
    codes = (blocks / scale).astype(np.float32).astype(dtype).astype(np.float64)
    return np.moveaxis((codes * scale).reshape(v.shape), -1, axis)


WIDE = False


def mx_kscale(k):
    if not WIDE:
        return np.ones(k)
    levels = np.array([10, -10, 5, -5, 0])
    if k % 512:
        return np.exp2(np.random.permutation(np.resize(levels, k // 32))).repeat(32)
    a = np.empty((k // 512, 16))
    for p in range(k // 512):
        a[p, :8] = np.random.permutation(np.resize(levels, 8))
        for g in range(8):
            far = levels[np.abs(levels - a[p, g]) >= 10]
            a[p, g + 8] = far[np.random.randint(len(far))]
    return np.exp2(a.ravel()).repeat(32)


def f64(x):
    return np.asarray(x).astype(np.float64)


def striped(idx):
    return np.tile(np.asarray(idx).reshape(-1, 16).T, (8, 1)).astype(np.uint16)


def unstriped(offs):
    return offs[:16].T.reshape(-1).astype(np.int64)


E2M1 = np.array([0.0, 0.5, 1.0, 1.5, 2.0, 3.0, 4.0, 6.0, -0.0, -0.5, -1.0, -1.5, -2.0, -3.0, -4.0, -6.0])


def pack_weight(w, fmt):
    k, n = w.shape
    w = f64(np.asarray(w, np.float32).astype(ml_dtypes.bfloat16)).reshape(k // 32, 32, n)
    amax = np.abs(w).max(1)
    if fmt == "e4m3":
        byte = np.frexp(amax)[1] - 1 + 127 - 7
    else:
        mant, ex = np.frexp(amax / 6.0)
        byte = np.where(mant > 0.5, ex, ex - 1) + 127
    byte = np.clip(np.where(amax > 0, byte, 1), 1, 254)
    scaled = (w * np.exp2(127.0 - byte)[:, None, :]).reshape(k, n).astype(np.float32)
    by_word = np.ascontiguousarray(scaled.reshape(k // 512, 128, 4, n).transpose(0, 1, 3, 2))
    if fmt == "e4m3":
        words = by_word.astype(ml_dtypes.float8_e4m3fn).view(np.uint8)
    else:
        c = by_word.astype(ml_dtypes.float4_e2m1fn).view(np.uint8) & 0xF
        words = (c[..., 0::2] | (c[..., 1::2] << 4)).reshape(k // 512, 128, 2 * n)
    return np.ascontiguousarray(words), np.ascontiguousarray(byte.astype(np.uint8).reshape(k // 512, 16, n))


def unpack_weight(words, scales, fmt):
    g, _, n = scales.shape
    words = np.ascontiguousarray(words).reshape(g, 128, n, -1)
    if fmt == "e4m3":
        vals = words.view(ml_dtypes.float8_e4m3fn).astype(np.float64)
    else:
        nib = np.empty((g, 128, n, 4), np.uint8)
        nib[..., 0::2] = words & 0xF
        nib[..., 1::2] = words >> 4
        vals = E2M1[nib]
    vals = vals * np.repeat(np.exp2(scales.astype(np.float64) - 127.0), 8, axis=1)[..., None]
    return vals.transpose(0, 1, 3, 2).reshape(g * 512, n)


D, E, T, I, G, U, Q = 512, 512, 4096, 1024, 64, 512, 128


def setup_inputs():
    n = np.random.standard_normal
    idx = np.random.permutation(T)[:I]
    idx2 = np.random.permutation(U)[:G]
    fd = mx_kscale(D)
    fe = mx_kscale(E)
    keysp = pack_weight(n((D, T)) / fd[:, None], "e4m3")
    valsp = pack_weight(n((E, T)) / fe[:, None], "e4m3")
    return {
        "query": (n((D, Q)) * 0.6 / np.sqrt(D) * fd[:, None]).astype(np.float32),
        "keys_words": keysp[0],
        "keys_scales": keysp[1],
        "pquery": (n((D, Q)) * 0.6 / np.sqrt(D) * fd[:, None]).astype(np.float32),
        "pgsum": (n((D, U)) / fd[:, None]).astype(np.float32),
        "gout": (n((E, Q)) * 1 / np.sqrt(E) * fe[:, None]).astype(np.float32),
        "vals_words": valsp[0],
        "vals_scales": valsp[1],
        "offs": striped(idx),
        "offs2": striped(idx2),
    }


def reference(query, keys_words, keys_scales, pquery, pgsum, gout, vals_words, vals_scales, offs, offs2):
    idx = unstriped(offs)
    idx2 = unstriped(offs2)
    keysu = unpack_weight(keys_words, keys_scales, "e4m3")
    valsu = unpack_weight(vals_words, vals_scales, "e4m3")
    pqueryq = mxq(f64(pquery), 0, "e4m3")
    pgsumq = mxq(f64(pgsum), 0, "e4m3")
    b = pqueryq.T @ pgsumq
    pb = np.exp(b - np.max(b, axis=1, keepdims=True))
    mb = pb / np.sum(pb, axis=1, keepdims=True)
    queryq = mxq(f64(query), 0, "e4m3")
    keysidxg = keysu[:, idx]
    a = queryq.T @ keysidxg
    pa = np.exp(a - np.max(a, axis=1, keepdims=True))
    goutq = mxq(f64(gout), 0, "e4m3")
    valsidxg = valsu[:, idx]
    dp = goutq.T @ valsidxg
    md = (pa * dp).reshape(Q, G, I // G).sum(axis=2) / pa.reshape(Q, G, I // G).sum(axis=2) * mb[:, idx2]
    mf = np.zeros((Q, U))
    mf[:, idx2] = md
    y = (mf - mb * np.sum(md, axis=1, keepdims=True)) * 256.0
    return y

@@ -1,0 +1,178 @@
+from contextlib import ExitStack
+
+import concourse.mybir as mybir
+
+D, T, I, G, U, Q = 512, 4096, 1024, 64, 512, 128
+FLOPS = 2 * D * Q * (U + 2 * I)
+
+F32 = mybir.dt.float32
+BF16 = mybir.dt.bfloat16
+I32 = mybir.dt.int32
+U32 = mybir.dt.uint32
+U16 = mybir.dt.uint16
+U8 = mybir.dt.uint8
+FP8X4 = mybir.dt.float8_e4m3fn_x4
+ALU = mybir.AluOpType
+ACT = mybir.ActivationFunctionType
+AX = mybir.AxisListType
+
+P = 128
+PACK = 4
+HALF = 512
+PAGE = I // G
+VALS_ROW = 4
+
+
+def tile_attend_gpagemass_kernel(tc, query, keys_words, keys_scales, pquery, pgsum, gout, vals_words, vals_scales, offs, offs2, out):
+    nc = tc.nc
+    with ExitStack() as ctx:
+        lists = ctx.enter_context(tc.tile_pool(name="lists", bufs=1))
+        sb = ctx.enter_context(tc.tile_pool(name="sb", bufs=1))
+        ps = ctx.enter_context(tc.psum_pool(name="ps", bufs=1))
+
+        slots = lists.tile([P, I // 16], U16, name="slots")
+        pages = lists.tile([P, G // 16], U16, name="pages")
+        nc.sync.dma_start(slots[:], offs)
+        nc.sync.dma_start(pages[:], offs2)
+
+        def load_rows(src, name, tag):
+            raw = sb.tile([P, PACK, src.shape[1]], F32, name=name, tag=tag, align_bytes=64)
+            nc.sync.dma_start(out=raw[:], in_=src.rearrange("(p j) c -> p j c", j=PACK))
+            return raw
+
+        def interleave(raw, name, tag):
+            width = raw.shape[2]
+            grouped = sb.tile([P, width * PACK], BF16, name=name, tag=tag, align_bytes=64)
+            nc.scalar.copy(
+                out=grouped[:].rearrange("p (c i t) -> p c t i", i=4, t=PACK),
+                in_=raw[:].rearrange("p t (c i) -> p c t i", i=4),
+            )
+            return grouped
+
+        def quantize(grouped, name):
+            width = grouped.shape[1] // PACK
+            codes = sb.tile([P, width], U32, name=name + "_codes", align_bytes=64)
+            scales = sb.tile([P, width], U8, name=name + "_scales", align_bytes=64)
+            nc.vector.quantize_mx(out=codes[:].bitcast(FP8X4), scales=scales[:], in_=grouped[:])
+            return codes, scales
+
+        def load_scales(src, name, row, queue):
+            pool_scales = sb.tile([P, T], U8, name=name, align_bytes=64)
+            as_words = pool_scales[:].bitcast(I32)
+            nc.vector.memset(as_words, 0)
+            for quad in range(4):
+                queue.dma_start(
+                    out=as_words[32 * quad + row : 32 * quad + row + 4, :],
+                    in_=src[0, 4 * quad : 4 * quad + 4, :].bitcast(I32),
+                )
+            return pool_scales
+
+        def load_words(src, name, tag):
+            pool_words = sb.tile([P, T], U32, name=name, tag=tag, align_bytes=64)
+            nc.sync.dma_start(
+                out=pool_words[:].bitcast(I32),
+                in_=src[0].rearrange("p n t -> p (n t)").bitcast(I32),
+            )
+            return pool_words
+
+        def gather_scales(pool_scales, name):
+            got = sb.tile([P, I], U8, name=name, align_bytes=64)
+            nc.vector.tensor_copy(got[:], pool_scales[:].indirect(slots[:]))
+            return got
+
+        def gather_words(pool_words, h, name):
+            got = sb.tile([P, HALF], U32, name=name, align_bytes=64)
+            nc.vector.tensor_copy(got[:], pool_words[:].indirect(slots[:, h * (HALF // 16) : (h + 1) * (HALF // 16)]))
+            return got
+
+        def product(name, stationary, words, scales):
+            bank = ps.tile([P, HALF], F32, name=name)
+            nc.tensor.matmul_mx(
+                out=bank[:],
+                lhsT=stationary[0][:].bitcast(FP8X4),
+                lhsT_scale=stationary[1][:],
+                rhs=words.bitcast(FP8X4),
+                rhs_scale=scales,
+                start=True,
+                stop=True,
+            )
+            return bank
+
+        keys_pool_scales = load_scales(keys_scales, "keys_pool_scales", 0, nc.scalar)
+        vals_pool_scales = load_scales(vals_scales, "vals_pool_scales", VALS_ROW, nc.gpsimd)
+        mf = sb.tile([P, U], F32, name="mf")
+        nc.vector.memset(mf[:], 0.0)
+        warm = sb.tile([P, 1], F32, name="warm")
+        nc.scalar.activation(warm[:], mf[:, 0:1], ACT.Exp)
+
+        q_raw = load_rows(query, "q_raw", "then_keys")
+        pq_raw = load_rows(pquery, "pq_raw", "then_gout")
+        pg_raw = load_rows(pgsum, "pg_raw", "pg_raw")
+        q_bf = interleave(q_raw, "q_bf", "q_bf")
+        pq_bf = interleave(pq_raw, "pq_bf", "then_vals")
+        q_mx = quantize(q_bf, "q")
+        pq_mx = quantize(pq_bf, "pq")
+        keys_pool = load_words(keys_words, "keys_pool", "then_keys")
+        g_raw = load_rows(gout, "g_raw", "then_gout")
+        vals_pool = load_words(vals_words, "vals_pool", "then_vals")
+
+        keys_sc = gather_scales(keys_pool_scales, "keys_sc")
+        vals_sc = gather_scales(vals_pool_scales, "vals_sc")
+
+        pg_bf = interleave(pg_raw, "pg_bf", "pg_bf")
+        pg_mx = quantize(pg_bf, "pg")
+        b = product("b", pq_mx, pg_mx[0][:], pg_mx[1][:])
+        neg_max_b = sb.tile([P, 1], F32, name="neg_max_b")
+        nc.vector.tensor_reduce(neg_max_b[:], b[:], AX.X, ALU.max, negate=True)
+        pb = sb.tile([P, U], F32, name="pb")
+        sum_b = sb.tile([P, 1], F32, name="sum_b")
+        nc.scalar.activation(pb[:], b[:], ACT.Exp, bias=neg_max_b[:], accum_out=sum_b[:])
+        inv_sum_b = sb.tile([P, 1], F32, name="inv_sum_b")
+        nc.vector.reciprocal(inv_sum_b[:], sum_b[:])
+        mb = sb.tile([P, U], F32, name="mb")
+        nc.scalar.activation(mb[:], pb[:], ACT.Copy, scale=inv_sum_b[:])
+
+        g_bf = interleave(g_raw, "g_bf", "g_bf")
+        g_mx = quantize(g_bf, "g")
+
+        den = sb.tile([P, G], F32, name="den")
+        keys_got = [gather_words(keys_pool, h, "keys_got%d" % h) for h in range(2)]
+        pa = []
+        for h in range(2):
+            a = product("a%d" % h, q_mx, keys_got[h][:], keys_sc[:, h * HALF : (h + 1) * HALF])
+            neg_max_a = sb.tile([P, 1], F32, name="neg_max_a%d" % h)
+            nc.vector.tensor_reduce(neg_max_a[:], a[:], AX.X, ALU.max, negate=True)
+            pa_h = sb.tile([P, HALF], F32, name="pa%d" % h)
+            nc.scalar.activation(pa_h[:], a[:], ACT.Exp, bias=neg_max_a[:])
+            pa.append(pa_h)
+        for h in range(2):
+            nc.vector.tensor_reduce(
+                den[:, h * (G // 2) : (h + 1) * (G // 2)], pa[h][:].rearrange("p (g j) -> p g j", j=PAGE), AX.X, ALU.add
+            )
+        inv_den = sb.tile([P, G], F32, name="inv_den")
+        nc.vector.reciprocal(inv_den[:], den[:])
+        factor = sb.tile([P, G], F32, name="factor")
+        nc.vector.tensor_tensor(factor[:], mb[:].indirect(pages[:]), inv_den[:], ALU.mult)
+
+        num = sb.tile([P, G], F32, name="num")
+        vals_got = [gather_words(vals_pool, h, "vals_got%d" % h) for h in range(2)]
+        prod = []
+        for h in range(2):
+            dp = product("dp%d" % h, g_mx, vals_got[h][:], vals_sc[VALS_ROW:P, h * HALF : (h + 1) * HALF])
+            prod_h = sb.tile([P, HALF], F32, name="prod%d" % h)
+            nc.vector.scalar_tensor_tensor(prod_h[:], dp[:], 256.0, pa[h][:], ALU.mult, ALU.mult)
+            prod.append(prod_h)
+        for h in range(2):
+            nc.vector.tensor_reduce(
+                num[:, h * (G // 2) : (h + 1) * (G // 2)], prod[h][:].rearrange("p (g j) -> p g j", j=PAGE), AX.X, ALU.add
+            )
+
+        neg_md = sb.tile([P, G], F32, name="neg_md")
+        neg_total = sb.tile([P, 1], F32, name="neg_total")
+        nc.vector.scalar_tensor_tensor(neg_md[:], num[:], -1.0, factor[:], ALU.mult, ALU.mult, accum_out=neg_total[:])
+        nc.vector.tensor_tensor(mf[:].indirect(pages[:]), num[:], factor[:], ALU.mult)
+        for h, queue in enumerate((nc.sync, nc.scalar)):
+            cols = slice(h * (U // 2), (h + 1) * (U // 2))
+            y = sb.tile([P, U // 2], F32, name="y%d" % h)
+            nc.vector.scalar_tensor_tensor(y[:], mb[:, cols], neg_total[:], mf[:, cols], ALU.mult, ALU.add)
+            queue.dma_start(out=out[:, cols], in_=y[:])

@@ -37,7 +37,7 @@ def tile_attend_gpagemass_kernel(tc, query, keys_words, keys_scales, pquery, pgs
 
         def load_rows(src, name, tag):
             raw = sb.tile([P, PACK, src.shape[1]], F32, name=name, tag=tag, align_bytes=64)
-            nc.sync.dma_start(out=raw[:], in_=src.rearrange("(p j) c -> p j c", j=PACK))
+            nc.scalar.dma_start(out=raw[:], in_=src.rearrange("(p j) c -> p j c", j=PACK))
             return raw
 
         def interleave(raw, name, tag):
@@ -49,9 +49,9 @@ def tile_attend_gpagemass_kernel(tc, query, keys_words, keys_scales, pquery, pgs
             )
             return grouped
 
-        def quantize(grouped, name):
+        def quantize(grouped, name, tag):
             width = grouped.shape[1] // PACK
-            codes = sb.tile([P, width], U32, name=name + "_codes", align_bytes=64)
+            codes = sb.tile([P, width], U32, name=name + "_codes", tag=tag, align_bytes=64)
             scales = sb.tile([P, width], U8, name=name + "_scales", align_bytes=64)
             nc.vector.quantize_mx(out=codes[:].bitcast(FP8X4), scales=scales[:], in_=grouped[:])
             return codes, scales
@@ -69,7 +69,7 @@ def tile_attend_gpagemass_kernel(tc, query, keys_words, keys_scales, pquery, pgs
 
         def load_words(src, name, tag):
             pool_words = sb.tile([P, T], U32, name=name, tag=tag, align_bytes=64)
-            nc.sync.dma_start(
+            nc.scalar.dma_start(
                 out=pool_words[:].bitcast(I32),
                 in_=src[0].rearrange("p n t -> p (n t)").bitcast(I32),
             )
@@ -80,10 +80,12 @@ def tile_attend_gpagemass_kernel(tc, query, keys_words, keys_scales, pquery, pgs
             nc.vector.tensor_copy(got[:], pool_scales[:].indirect(slots[:]))
             return got
 
-        def gather_words(pool_words, h, name):
-            got = sb.tile([P, HALF], U32, name=name, align_bytes=64)
-            nc.vector.tensor_copy(got[:], pool_words[:].indirect(slots[:, h * (HALF // 16) : (h + 1) * (HALF // 16)]))
-            return got
+        def gather_words(pool_words, name, tag):
+            got = sb.tile([P, I], U32, name=name, tag=tag, align_bytes=64)
+            halves = [got[:, h * HALF : (h + 1) * HALF] for h in range(2)]
+            for h in range(2):
+                nc.vector.tensor_copy(halves[h], pool_words[:].indirect(slots[:, h * (HALF // 16) : (h + 1) * (HALF // 16)]))
+            return halves
 
         def product(name, stationary, words, scales):
             bank = ps.tile([P, HALF], F32, name=name)
@@ -98,29 +100,31 @@ def tile_attend_gpagemass_kernel(tc, query, keys_words, keys_scales, pquery, pgs
             )
             return bank
 
-        keys_pool_scales = load_scales(keys_scales, "keys_pool_scales", 0, nc.scalar)
-        vals_pool_scales = load_scales(vals_scales, "vals_pool_scales", VALS_ROW, nc.gpsimd)
+        keys_pool_scales = load_scales(keys_scales, "keys_pool_scales", 0, nc.sync)
+        vals_pool_scales = load_scales(vals_scales, "vals_pool_scales", VALS_ROW, nc.sync)
         mf = sb.tile([P, U], F32, name="mf")
         nc.vector.memset(mf[:], 0.0)
-        warm = sb.tile([P, 1], F32, name="warm")
-        nc.scalar.activation(warm[:], mf[:, 0:1], ACT.Exp)
+        warm = sb.tile([P, 1], F32, name="warm", tag="then_pquery", align_bytes=64)
+        nc.gpsimd.memset(warm[:], 0.0)
+        warm_out = sb.tile([P, 1], F32, name="warm_out")
 
         q_raw = load_rows(query, "q_raw", "then_keys")
-        pq_raw = load_rows(pquery, "pq_raw", "then_gout")
-        pg_raw = load_rows(pgsum, "pg_raw", "pg_raw")
+        pg_raw = load_rows(pgsum, "pg_raw", "then_vals")
+        nc.scalar.activation(warm_out[:], warm[:], ACT.Exp)
+        pq_raw = load_rows(pquery, "pq_raw", "then_pquery")
         q_bf = interleave(q_raw, "q_bf", "q_bf")
-        pq_bf = interleave(pq_raw, "pq_bf", "then_vals")
-        q_mx = quantize(q_bf, "q")
-        pq_mx = quantize(pq_bf, "pq")
         keys_pool = load_words(keys_words, "keys_pool", "then_keys")
-        g_raw = load_rows(gout, "g_raw", "then_gout")
+        pq_bf = interleave(pq_raw, "pq_bf", "pq_bf")
+        g_raw = load_rows(gout, "g_raw", "then_pquery")
+        pg_bf = interleave(pg_raw, "pg_bf", "pg_bf")
         vals_pool = load_words(vals_words, "vals_pool", "then_vals")
+        q_mx = quantize(q_bf, "q", "q_codes")
+        pq_mx = quantize(pq_bf, "pq", "pq_codes")
 
         keys_sc = gather_scales(keys_pool_scales, "keys_sc")
         vals_sc = gather_scales(vals_pool_scales, "vals_sc")
 
-        pg_bf = interleave(pg_raw, "pg_bf", "pg_bf")
-        pg_mx = quantize(pg_bf, "pg")
+        pg_mx = quantize(pg_bf, "pg", "then_keys_got")
         b = product("b", pq_mx, pg_mx[0][:], pg_mx[1][:])
         neg_max_b = sb.tile([P, 1], F32, name="neg_max_b")
         nc.vector.tensor_reduce(neg_max_b[:], b[:], AX.X, ALU.max, negate=True)
@@ -132,14 +136,11 @@ def tile_attend_gpagemass_kernel(tc, query, keys_words, keys_scales, pquery, pgs
         mb = sb.tile([P, U], F32, name="mb")
         nc.scalar.activation(mb[:], pb[:], ACT.Copy, scale=inv_sum_b[:])
 
-        g_bf = interleave(g_raw, "g_bf", "g_bf")
-        g_mx = quantize(g_bf, "g")
-
         den = sb.tile([P, G], F32, name="den")
-        keys_got = [gather_words(keys_pool, h, "keys_got%d" % h) for h in range(2)]
+        keys_got = gather_words(keys_pool, "keys_got", "then_keys_got")
         pa = []
         for h in range(2):
-            a = product("a%d" % h, q_mx, keys_got[h][:], keys_sc[:, h * HALF : (h + 1) * HALF])
+            a = product("a%d" % h, q_mx, keys_got[h], keys_sc[:, h * HALF : (h + 1) * HALF])
             neg_max_a = sb.tile([P, 1], F32, name="neg_max_a%d" % h)
             nc.vector.tensor_reduce(neg_max_a[:], a[:], AX.X, ALU.max, negate=True)
             pa_h = sb.tile([P, HALF], F32, name="pa%d" % h)
@@ -149,16 +150,18 @@ def tile_attend_gpagemass_kernel(tc, query, keys_words, keys_scales, pquery, pgs
             nc.vector.tensor_reduce(
                 den[:, h * (G // 2) : (h + 1) * (G // 2)], pa[h][:].rearrange("p (g j) -> p g j", j=PAGE), AX.X, ALU.add
             )
-        inv_den = sb.tile([P, G], F32, name="inv_den")
+        g_bf = interleave(g_raw, "g_bf", "g_bf")
+        g_mx = quantize(g_bf, "g", "g_codes")
+        inv_den = sb.tile([P, G], F32, name="inv_den", tag="then_vals_got", align_bytes=64)
         nc.vector.reciprocal(inv_den[:], den[:])
         factor = sb.tile([P, G], F32, name="factor")
         nc.vector.tensor_tensor(factor[:], mb[:].indirect(pages[:]), inv_den[:], ALU.mult)
 
         num = sb.tile([P, G], F32, name="num")
-        vals_got = [gather_words(vals_pool, h, "vals_got%d" % h) for h in range(2)]
+        vals_got = gather_words(vals_pool, "vals_got", "then_vals_got")
         prod = []
         for h in range(2):
-            dp = product("dp%d" % h, g_mx, vals_got[h][:], vals_sc[VALS_ROW:P, h * HALF : (h + 1) * HALF])
+            dp = product("dp%d" % h, g_mx, vals_got[h], vals_sc[VALS_ROW:P, h * HALF : (h + 1) * HALF])
             prod_h = sb.tile([P, HALF], F32, name="prod%d" % h)
             nc.vector.scalar_tensor_tensor(prod_h[:], dp[:], 256.0, pa[h][:], ALU.mult, ALU.mult)
             prod.append(prod_h)

@@ -37,7 +37,7 @@ def tile_attend_gpagemass_kernel(tc, query, keys_words, keys_scales, pquery, pgs
 
         def load_rows(src, name, tag):
             raw = sb.tile([P, PACK, src.shape[1]], F32, name=name, tag=tag, align_bytes=64)
-            nc.scalar.dma_start(out=raw[:], in_=src.rearrange("(p j) c -> p j c", j=PACK))
+            nc.sync.dma_start(out=raw[:], in_=src.rearrange("(p j) c -> p j c", j=PACK))
             return raw
 
         def interleave(raw, name, tag):
@@ -49,19 +49,19 @@ def tile_attend_gpagemass_kernel(tc, query, keys_words, keys_scales, pquery, pgs
             )
             return grouped
 
-        def quantize(grouped, name, tag):
+        def quantize(grouped, name, tag, scales_tag):
             width = grouped.shape[1] // PACK
             codes = sb.tile([P, width], U32, name=name + "_codes", tag=tag, align_bytes=64)
-            scales = sb.tile([P, width], U8, name=name + "_scales", align_bytes=64)
+            scales = sb.tile([P, width], U8, name=name + "_scales", tag=scales_tag, align_bytes=64)
             nc.vector.quantize_mx(out=codes[:].bitcast(FP8X4), scales=scales[:], in_=grouped[:])
             return codes, scales
 
-        def load_scales(src, name, row, queue):
-            pool_scales = sb.tile([P, T], U8, name=name, align_bytes=64)
+        def load_scales(src, name, row, tag):
+            pool_scales = sb.tile([P, T], U8, name=name, tag=tag, align_bytes=64)
             as_words = pool_scales[:].bitcast(I32)
             nc.vector.memset(as_words, 0)
             for quad in range(4):
-                queue.dma_start(
+                nc.sync.dma_start(
                     out=as_words[32 * quad + row : 32 * quad + row + 4, :],
                     in_=src[0, 4 * quad : 4 * quad + 4, :].bitcast(I32),
                 )
@@ -69,7 +69,7 @@ def tile_attend_gpagemass_kernel(tc, query, keys_words, keys_scales, pquery, pgs
 
         def load_words(src, name, tag):
             pool_words = sb.tile([P, T], U32, name=name, tag=tag, align_bytes=64)
-            nc.scalar.dma_start(
+            nc.sync.dma_start(
                 out=pool_words[:].bitcast(I32),
                 in_=src[0].rearrange("p n t -> p (n t)").bitcast(I32),
             )
@@ -100,33 +100,33 @@ def tile_attend_gpagemass_kernel(tc, query, keys_words, keys_scales, pquery, pgs
             )
             return bank
 
-        keys_pool_scales = load_scales(keys_scales, "keys_pool_scales", 0, nc.sync)
-        vals_pool_scales = load_scales(vals_scales, "vals_pool_scales", VALS_ROW, nc.sync)
+        keys_pool_scales = load_scales(keys_scales, "keys_pool_scales", 0, "then_gout")
         mf = sb.tile([P, U], F32, name="mf")
         nc.vector.memset(mf[:], 0.0)
-        warm = sb.tile([P, 1], F32, name="warm", tag="then_pquery", align_bytes=64)
+        warm = sb.tile([P, 1], F32, name="warm", tag="then_pgsum", align_bytes=64)
         nc.gpsimd.memset(warm[:], 0.0)
-        warm_out = sb.tile([P, 1], F32, name="warm_out")
+        warm_out = sb.tile([P, 1], F32, name="warm_out", tag="then_vals_scales", align_bytes=64)
 
-        q_raw = load_rows(query, "q_raw", "then_keys")
-        pg_raw = load_rows(pgsum, "pg_raw", "then_vals")
+        q_raw = load_rows(query, "q_raw", "q_raw")
+        pq_raw = load_rows(pquery, "pq_raw", "then_keys")
         nc.scalar.activation(warm_out[:], warm[:], ACT.Exp)
-        pq_raw = load_rows(pquery, "pq_raw", "then_pquery")
+        pg_raw = load_rows(pgsum, "pg_raw", "then_pgsum")
+        vals_pool_scales = load_scales(vals_scales, "vals_pool_scales", VALS_ROW, "then_vals_scales")
         q_bf = interleave(q_raw, "q_bf", "q_bf")
-        keys_pool = load_words(keys_words, "keys_pool", "then_keys")
         pq_bf = interleave(pq_raw, "pq_bf", "pq_bf")
-        g_raw = load_rows(gout, "g_raw", "then_pquery")
-        pg_bf = interleave(pg_raw, "pg_bf", "pg_bf")
-        vals_pool = load_words(vals_words, "vals_pool", "then_vals")
-        q_mx = quantize(q_bf, "q", "q_codes")
-        pq_mx = quantize(pq_bf, "pq", "pq_codes")
-
+        keys_pool = load_words(keys_words, "keys_pool", "then_keys")
+        q_mx = quantize(q_bf, "q", "q_codes", "q_scales")
+        pq_mx = quantize(pq_bf, "pq", "pq_codes", "pq_scales")
         keys_sc = gather_scales(keys_pool_scales, "keys_sc")
+        g_raw = load_rows(gout, "g_raw", "then_gout")
+        pg_bf = interleave(pg_raw, "pg_bf", "then_keys_got")
+        vals_pool = load_words(vals_words, "vals_pool", "then_pgsum")
         vals_sc = gather_scales(vals_pool_scales, "vals_sc")
 
-        pg_mx = quantize(pg_bf, "pg", "then_keys_got")
+        pg_mx = quantize(pg_bf, "pg", "pg_codes", "then_vals_scales")
         b = product("b", pq_mx, pg_mx[0][:], pg_mx[1][:])
-        neg_max_b = sb.tile([P, 1], F32, name="neg_max_b")
+        keys_got = gather_words(keys_pool, "keys_got", "then_keys_got")
+        neg_max_b = sb.tile([P, 1], F32, name="neg_max_b", tag="then_keys", align_bytes=64)
         nc.vector.tensor_reduce(neg_max_b[:], b[:], AX.X, ALU.max, negate=True)
         pb = sb.tile([P, U], F32, name="pb")
         sum_b = sb.tile([P, 1], F32, name="sum_b")
@@ -137,11 +137,10 @@ def tile_attend_gpagemass_kernel(tc, query, keys_words, keys_scales, pquery, pgs
         nc.scalar.activation(mb[:], pb[:], ACT.Copy, scale=inv_sum_b[:])
 
         den = sb.tile([P, G], F32, name="den")
-        keys_got = gather_words(keys_pool, "keys_got", "then_keys_got")
         pa = []
         for h in range(2):
             a = product("a%d" % h, q_mx, keys_got[h], keys_sc[:, h * HALF : (h + 1) * HALF])
-            neg_max_a = sb.tile([P, 1], F32, name="neg_max_a%d" % h)
+            neg_max_a = sb.tile([P, 1], F32, name="neg_max_a%d" % h, tag=("neg_max_a0", "then_vals_got")[h], align_bytes=64)
             nc.vector.tensor_reduce(neg_max_a[:], a[:], AX.X, ALU.max, negate=True)
             pa_h = sb.tile([P, HALF], F32, name="pa%d" % h)
             nc.scalar.activation(pa_h[:], a[:], ACT.Exp, bias=neg_max_a[:])
@@ -151,14 +150,14 @@ def tile_attend_gpagemass_kernel(tc, query, keys_words, keys_scales, pquery, pgs
                 den[:, h * (G // 2) : (h + 1) * (G // 2)], pa[h][:].rearrange("p (g j) -> p g j", j=PAGE), AX.X, ALU.add
             )
         g_bf = interleave(g_raw, "g_bf", "g_bf")
-        g_mx = quantize(g_bf, "g", "g_codes")
-        inv_den = sb.tile([P, G], F32, name="inv_den", tag="then_vals_got", align_bytes=64)
+        g_mx = quantize(g_bf, "g", "g_codes", "g_scales")
+        vals_got = gather_words(vals_pool, "vals_got", "then_vals_got")
+        inv_den = sb.tile([P, G], F32, name="inv_den", tag="then_pgsum", align_bytes=64)
         nc.vector.reciprocal(inv_den[:], den[:])
         factor = sb.tile([P, G], F32, name="factor")
         nc.vector.tensor_tensor(factor[:], mb[:].indirect(pages[:]), inv_den[:], ALU.mult)
 
         num = sb.tile([P, G], F32, name="num")
-        vals_got = gather_words(vals_pool, "vals_got", "then_vals_got")
         prod = []
         for h in range(2):
             dp = product("dp%d" % h, g_mx, vals_got[h], vals_sc[VALS_ROW:P, h * HALF : (h + 1) * HALF])
@@ -170,10 +169,10 @@ def tile_attend_gpagemass_kernel(tc, query, keys_words, keys_scales, pquery, pgs
                 num[:, h * (G // 2) : (h + 1) * (G // 2)], prod[h][:].rearrange("p (g j) -> p g j", j=PAGE), AX.X, ALU.add
             )
 
+        nc.vector.tensor_tensor(mf[:].indirect(pages[:]), num[:], factor[:], ALU.mult)
         neg_md = sb.tile([P, G], F32, name="neg_md")
         neg_total = sb.tile([P, 1], F32, name="neg_total")
         nc.vector.scalar_tensor_tensor(neg_md[:], num[:], -1.0, factor[:], ALU.mult, ALU.mult, accum_out=neg_total[:])
-        nc.vector.tensor_tensor(mf[:].indirect(pages[:]), num[:], factor[:], ALU.mult)
         for h, queue in enumerate((nc.sync, nc.scalar)):
             cols = slice(h * (U // 2), (h + 1) * (U // 2))
             y = sb.tile([P, U // 2], F32, name="y%d" % h)

@@ -60,11 +60,9 @@ def tile_attend_gpagemass_kernel(tc, query, keys_words, keys_scales, pquery, pgs
             pool_scales = sb.tile([P, T], U8, name=name, tag=tag, align_bytes=64)
             as_words = pool_scales[:].bitcast(I32)
             nc.vector.memset(as_words, 0)
-            for quad in range(4):
-                nc.sync.dma_start(
-                    out=as_words[32 * quad + row : 32 * quad + row + 4, :],
-                    in_=src[0, 4 * quad : 4 * quad + 4, :].bitcast(I32),
-                )
+            rows = src[0].rearrange("(quad j) n -> j quad n", j=4)
+            for j in range(4):
+                nc.sync.dma_start(out=as_words[row + j : P : 32, :], in_=rows[j].bitcast(I32))
             return pool_scales
 
         def load_words(src, name, tag):
@@ -131,10 +129,6 @@ def tile_attend_gpagemass_kernel(tc, query, keys_words, keys_scales, pquery, pgs
         pb = sb.tile([P, U], F32, name="pb")
         sum_b = sb.tile([P, 1], F32, name="sum_b")
         nc.scalar.activation(pb[:], b[:], ACT.Exp, bias=neg_max_b[:], accum_out=sum_b[:])
-        inv_sum_b = sb.tile([P, 1], F32, name="inv_sum_b")
-        nc.vector.reciprocal(inv_sum_b[:], sum_b[:])
-        mb = sb.tile([P, U], F32, name="mb")
-        nc.scalar.activation(mb[:], pb[:], ACT.Copy, scale=inv_sum_b[:])
 
         den = sb.tile([P, G], F32, name="den")
         pa = []
@@ -149,6 +143,10 @@ def tile_attend_gpagemass_kernel(tc, query, keys_words, keys_scales, pquery, pgs
             nc.vector.tensor_reduce(
                 den[:, h * (G // 2) : (h + 1) * (G // 2)], pa[h][:].rearrange("p (g j) -> p g j", j=PAGE), AX.X, ALU.add
             )
+        inv_sum_b = sb.tile([P, 1], F32, name="inv_sum_b", tag="neg_max_a0", align_bytes=64)
+        nc.vector.reciprocal(inv_sum_b[:], sum_b[:])
+        mb = sb.tile([P, U], F32, name="mb")
+        nc.scalar.activation(mb[:], pb[:], ACT.Copy, scale=inv_sum_b[:])
         g_bf = interleave(g_raw, "g_bf", "g_bf")
         g_mx = quantize(g_bf, "g", "g_codes", "g_scales")
         vals_got = gather_words(vals_pool, "vals_got", "then_vals_got")

@@ -40,13 +40,15 @@ def tile_attend_gpagemass_kernel(tc, query, keys_words, keys_scales, pquery, pgs
             nc.sync.dma_start(out=raw[:], in_=src.rearrange("(p j) c -> p j c", j=PACK))
             return raw
 
-        def interleave(raw, name, tag):
+        def interleave(raw, name, tag, copies):
             width = raw.shape[2]
+            share = width // len(copies)
             grouped = sb.tile([P, width * PACK], BF16, name=name, tag=tag, align_bytes=64)
-            nc.scalar.copy(
-                out=grouped[:].rearrange("p (c i t) -> p c t i", i=4, t=PACK),
-                in_=raw[:].rearrange("p t (c i) -> p c t i", i=4),
-            )
+            for n, copy in enumerate(copies):
+                copy(
+                    out=grouped[:, n * share * PACK : (n + 1) * share * PACK].rearrange("p (c i t) -> p c t i", i=4, t=PACK),
+                    in_=raw[:, :, n * share : (n + 1) * share].rearrange("p t (c i) -> p c t i", i=4),
+                )
             return grouped
 
         def quantize(grouped, name, tag, scales_tag):
@@ -98,43 +100,37 @@ def tile_attend_gpagemass_kernel(tc, query, keys_words, keys_scales, pquery, pgs
             )
             return bank
 
-        keys_pool_scales = load_scales(keys_scales, "keys_pool_scales", 0, "then_gout")
+        keys_pool_scales = load_scales(keys_scales, "keys_pool_scales", 0, "then_vals")
+        vals_pool_scales = load_scales(vals_scales, "vals_pool_scales", VALS_ROW, "then_keys_got")
         mf = sb.tile([P, U], F32, name="mf")
         nc.vector.memset(mf[:], 0.0)
-        warm = sb.tile([P, 1], F32, name="warm", tag="then_pgsum", align_bytes=64)
+        warm = sb.tile([P, 1], F32, name="warm", tag="then_keys", align_bytes=64)
         nc.gpsimd.memset(warm[:], 0.0)
-        warm_out = sb.tile([P, 1], F32, name="warm_out", tag="then_vals_scales", align_bytes=64)
+        warm_out = sb.tile([P, 1], F32, name="warm_out")
 
-        q_raw = load_rows(query, "q_raw", "q_raw")
-        pq_raw = load_rows(pquery, "pq_raw", "then_keys")
+        on_scalar = [nc.scalar.copy]
+        q_raw = load_rows(query, "q_raw", "then_gout")
+        pq_raw = load_rows(pquery, "pq_raw", "then_pgsum")
         nc.scalar.activation(warm_out[:], warm[:], ACT.Exp)
-        pg_raw = load_rows(pgsum, "pg_raw", "then_pgsum")
-        vals_pool_scales = load_scales(vals_scales, "vals_pool_scales", VALS_ROW, "then_vals_scales")
-        q_bf = interleave(q_raw, "q_bf", "q_bf")
-        pq_bf = interleave(pq_raw, "pq_bf", "pq_bf")
         keys_pool = load_words(keys_words, "keys_pool", "then_keys")
+        q_bf = interleave(q_raw, "q_bf", "q_bf", on_scalar)
+        g_raw = load_rows(gout, "g_raw", "then_gout")
+        pq_bf = interleave(pq_raw, "pq_bf", "pq_bf", on_scalar)
+        pg_raw = load_rows(pgsum, "pg_raw", "then_pgsum")
         q_mx = quantize(q_bf, "q", "q_codes", "q_scales")
         pq_mx = quantize(pq_bf, "pq", "pq_codes", "pq_scales")
         keys_sc = gather_scales(keys_pool_scales, "keys_sc")
-        g_raw = load_rows(gout, "g_raw", "then_gout")
-        pg_bf = interleave(pg_raw, "pg_bf", "then_keys_got")
-        vals_pool = load_words(vals_words, "vals_pool", "then_pgsum")
+        vals_pool = load_words(vals_words, "vals_pool", "then_vals")
         vals_sc = gather_scales(vals_pool_scales, "vals_sc")
-
-        pg_mx = quantize(pg_bf, "pg", "pg_codes", "then_vals_scales")
-        b = product("b", pq_mx, pg_mx[0][:], pg_mx[1][:])
         keys_got = gather_words(keys_pool, "keys_got", "then_keys_got")
-        neg_max_b = sb.tile([P, 1], F32, name="neg_max_b", tag="then_keys", align_bytes=64)
-        nc.vector.tensor_reduce(neg_max_b[:], b[:], AX.X, ALU.max, negate=True)
-        pb = sb.tile([P, U], F32, name="pb")
-        sum_b = sb.tile([P, 1], F32, name="sum_b")
-        nc.scalar.activation(pb[:], b[:], ACT.Exp, bias=neg_max_b[:], accum_out=sum_b[:])
+        g_bf = interleave(g_raw, "g_bf", "g_bf", on_scalar)
+        g_mx = quantize(g_bf, "g", "g_codes", "g_scales")
 
         den = sb.tile([P, G], F32, name="den")
         pa = []
         for h in range(2):
             a = product("a%d" % h, q_mx, keys_got[h], keys_sc[:, h * HALF : (h + 1) * HALF])
-            neg_max_a = sb.tile([P, 1], F32, name="neg_max_a%d" % h, tag=("neg_max_a0", "then_vals_got")[h], align_bytes=64)
+            neg_max_a = sb.tile([P, 1], F32, name="neg_max_a%d" % h)
             nc.vector.tensor_reduce(neg_max_a[:], a[:], AX.X, ALU.max, negate=True)
             pa_h = sb.tile([P, HALF], F32, name="pa%d" % h)
             nc.scalar.activation(pa_h[:], a[:], ACT.Exp, bias=neg_max_a[:])
@@ -143,15 +139,22 @@ def tile_attend_gpagemass_kernel(tc, query, keys_words, keys_scales, pquery, pgs
             nc.vector.tensor_reduce(
                 den[:, h * (G // 2) : (h + 1) * (G // 2)], pa[h][:].rearrange("p (g j) -> p g j", j=PAGE), AX.X, ALU.add
             )
-        inv_sum_b = sb.tile([P, 1], F32, name="inv_sum_b", tag="neg_max_a0", align_bytes=64)
+        inv_den = sb.tile([P, G], F32, name="inv_den")
+        nc.vector.reciprocal(inv_den[:], den[:])
+
+        pg_bf = interleave(pg_raw, "pg_bf", "then_vals_got", [nc.scalar.copy, nc.vector.tensor_copy])
+        pg_mx = quantize(pg_bf, "pg", "pg_codes", "pg_scales")
+        b = product("b", pq_mx, pg_mx[0][:], pg_mx[1][:])
+        vals_got = gather_words(vals_pool, "vals_got", "then_vals_got")
+        neg_max_b = sb.tile([P, 1], F32, name="neg_max_b", tag="then_vals", align_bytes=64)
+        nc.vector.tensor_reduce(neg_max_b[:], b[:], AX.X, ALU.max, negate=True)
+        pb = sb.tile([P, U], F32, name="pb")
+        sum_b = sb.tile([P, 1], F32, name="sum_b")
+        nc.scalar.activation(pb[:], b[:], ACT.Exp, bias=neg_max_b[:], accum_out=sum_b[:])
+        inv_sum_b = sb.tile([P, 1], F32, name="inv_sum_b")
         nc.vector.reciprocal(inv_sum_b[:], sum_b[:])
         mb = sb.tile([P, U], F32, name="mb")
         nc.scalar.activation(mb[:], pb[:], ACT.Copy, scale=inv_sum_b[:])
-        g_bf = interleave(g_raw, "g_bf", "g_bf")
-        g_mx = quantize(g_bf, "g", "g_codes", "g_scales")
-        vals_got = gather_words(vals_pool, "vals_got", "then_vals_got")
-        inv_den = sb.tile([P, G], F32, name="inv_den", tag="then_pgsum", align_bytes=64)
-        nc.vector.reciprocal(inv_den[:], den[:])
         factor = sb.tile([P, G], F32, name="factor")
         nc.vector.tensor_tensor(factor[:], mb[:].indirect(pages[:]), inv_den[:], ALU.mult)
 

from contextlib import ExitStack

import concourse.mybir as mybir

D, T, I, G, U, Q = 512, 4096, 1024, 64, 512, 128
FLOPS = 2 * D * Q * (U + 2 * I)

F32 = mybir.dt.float32
BF16 = mybir.dt.bfloat16
I32 = mybir.dt.int32
U32 = mybir.dt.uint32
U16 = mybir.dt.uint16
U8 = mybir.dt.uint8
FP8X4 = mybir.dt.float8_e4m3fn_x4
ALU = mybir.AluOpType
ACT = mybir.ActivationFunctionType
AX = mybir.AxisListType

P = 128
PACK = 4
HALF = 512
PAGE = I // G
VALS_ROW = 4


def tile_attend_gpagemass_kernel(tc, query, keys_words, keys_scales, pquery, pgsum, gout, vals_words, vals_scales, offs, offs2, out):
    nc = tc.nc
    with ExitStack() as ctx:
        lists = ctx.enter_context(tc.tile_pool(name="lists", bufs=1))
        sb = ctx.enter_context(tc.tile_pool(name="sb", bufs=1))
        ps = ctx.enter_context(tc.psum_pool(name="ps", bufs=1))

        slots = lists.tile([P, I // 16], U16, name="slots")
        pages = lists.tile([P, G // 16], U16, name="pages")
        nc.sync.dma_start(slots[:], offs)
        nc.sync.dma_start(pages[:], offs2)

        def load_rows(src, name, tag):
            raw = sb.tile([P, PACK, src.shape[1]], F32, name=name, tag=tag, align_bytes=64)
            nc.sync.dma_start(out=raw[:], in_=src.rearrange("(p j) c -> p j c", j=PACK))
            return raw

        def interleave(raw, name, tag, copies):
            width = raw.shape[2]
            share = width // len(copies)
            grouped = sb.tile([P, width * PACK], BF16, name=name, tag=tag, align_bytes=64)
            for n, copy in enumerate(copies):
                copy(
                    out=grouped[:, n * share * PACK : (n + 1) * share * PACK].rearrange("p (c i t) -> p c t i", i=4, t=PACK),
                    in_=raw[:, :, n * share : (n + 1) * share].rearrange("p t (c i) -> p c t i", i=4),
                )
            return grouped

        def quantize(grouped, name, tag, scales_tag):
            width = grouped.shape[1] // PACK
            codes = sb.tile([P, width], U32, name=name + "_codes", tag=tag, align_bytes=64)
            scales = sb.tile([P, width], U8, name=name + "_scales", tag=scales_tag, align_bytes=64)
            nc.vector.quantize_mx(out=codes[:].bitcast(FP8X4), scales=scales[:], in_=grouped[:])
            return codes, scales

        def load_scales(src, name, row, tag):
            pool_scales = sb.tile([P, T], U8, name=name, tag=tag, align_bytes=64)
            as_words = pool_scales[:].bitcast(I32)
            nc.vector.memset(as_words, 0)
            rows = src[0].rearrange("(quad j) n -> j quad n", j=4)
            for j in range(4):
                nc.sync.dma_start(out=as_words[row + j : P : 32, :], in_=rows[j].bitcast(I32))
            return pool_scales

        def load_words(src, name, tag):
            pool_words = sb.tile([P, T], U32, name=name, tag=tag, align_bytes=64)
            nc.sync.dma_start(
                out=pool_words[:].bitcast(I32),
                in_=src[0].rearrange("p n t -> p (n t)").bitcast(I32),
            )
            return pool_words

        def gather_scales(pool_scales, name):
            got = sb.tile([P, I], U8, name=name, align_bytes=64)
            nc.vector.tensor_copy(got[:], pool_scales[:].indirect(slots[:]))
            return got

        def gather_words(pool_words, name, tag):
            got = sb.tile([P, I], U32, name=name, tag=tag, align_bytes=64)
            halves = [got[:, h * HALF : (h + 1) * HALF] for h in range(2)]
            for h in range(2):
                nc.vector.tensor_copy(halves[h], pool_words[:].indirect(slots[:, h * (HALF // 16) : (h + 1) * (HALF // 16)]))
            return halves

        def product(name, stationary, words, scales):
            bank = ps.tile([P, HALF], F32, name=name)
            nc.tensor.matmul_mx(
                out=bank[:],
                lhsT=stationary[0][:].bitcast(FP8X4),
                lhsT_scale=stationary[1][:],
                rhs=words.bitcast(FP8X4),
                rhs_scale=scales,
                start=True,
                stop=True,
            )
            return bank

        keys_pool_scales = load_scales(keys_scales, "keys_pool_scales", 0, "then_vals")
        vals_pool_scales = load_scales(vals_scales, "vals_pool_scales", VALS_ROW, "then_keys_got")
        mf = sb.tile([P, U], F32, name="mf")
        nc.vector.memset(mf[:], 0.0)
        warm = sb.tile([P, 1], F32, name="warm", tag="then_keys", align_bytes=64)
        nc.gpsimd.memset(warm[:], 0.0)
        warm_out = sb.tile([P, 1], F32, name="warm_out")

        on_scalar = [nc.scalar.copy]
        q_raw = load_rows(query, "q_raw", "then_gout")
        pq_raw = load_rows(pquery, "pq_raw", "then_pgsum")
        nc.scalar.activation(warm_out[:], warm[:], ACT.Exp)
        keys_pool = load_words(keys_words, "keys_pool", "then_keys")
        q_bf = interleave(q_raw, "q_bf", "q_bf", on_scalar)
        g_raw = load_rows(gout, "g_raw", "then_gout")
        pq_bf = interleave(pq_raw, "pq_bf", "pq_bf", on_scalar)
        pg_raw = load_rows(pgsum, "pg_raw", "then_pgsum")
        q_mx = quantize(q_bf, "q", "q_codes", "q_scales")
        pq_mx = quantize(pq_bf, "pq", "pq_codes", "pq_scales")
        keys_sc = gather_scales(keys_pool_scales, "keys_sc")
        vals_pool = load_words(vals_words, "vals_pool", "then_vals")
        vals_sc = gather_scales(vals_pool_scales, "vals_sc")
        keys_got = gather_words(keys_pool, "keys_got", "then_keys_got")
        g_bf = interleave(g_raw, "g_bf", "g_bf", on_scalar)
        g_mx = quantize(g_bf, "g", "g_codes", "g_scales")

        den = sb.tile([P, G], F32, name="den")
        pa = []
        for h in range(2):
            a = product("a%d" % h, q_mx, keys_got[h], keys_sc[:, h * HALF : (h + 1) * HALF])
            neg_max_a = sb.tile([P, 1], F32, name="neg_max_a%d" % h)
            nc.vector.tensor_reduce(neg_max_a[:], a[:], AX.X, ALU.max, negate=True)
            pa_h = sb.tile([P, HALF], F32, name="pa%d" % h)
            nc.scalar.activation(pa_h[:], a[:], ACT.Exp, bias=neg_max_a[:])
            pa.append(pa_h)
        for h in range(2):
            nc.vector.tensor_reduce(
                den[:, h * (G // 2) : (h + 1) * (G // 2)], pa[h][:].rearrange("p (g j) -> p g j", j=PAGE), AX.X, ALU.add
            )
        inv_den = sb.tile([P, G], F32, name="inv_den")
        nc.vector.reciprocal(inv_den[:], den[:])

        pg_bf = interleave(pg_raw, "pg_bf", "then_vals_got", [nc.scalar.copy, nc.vector.tensor_copy])
        pg_mx = quantize(pg_bf, "pg", "pg_codes", "pg_scales")
        b = product("b", pq_mx, pg_mx[0][:], pg_mx[1][:])
        vals_got = gather_words(vals_pool, "vals_got", "then_vals_got")
        neg_max_b = sb.tile([P, 1], F32, name="neg_max_b", tag="then_vals", align_bytes=64)
        nc.vector.tensor_reduce(neg_max_b[:], b[:], AX.X, ALU.max, negate=True)
        pb = sb.tile([P, U], F32, name="pb")
        sum_b = sb.tile([P, 1], F32, name="sum_b")
        nc.scalar.activation(pb[:], b[:], ACT.Exp, bias=neg_max_b[:], accum_out=sum_b[:])
        inv_sum_b = sb.tile([P, 1], F32, name="inv_sum_b")
        nc.vector.reciprocal(inv_sum_b[:], sum_b[:])
        mb = sb.tile([P, U], F32, name="mb")
        nc.scalar.activation(mb[:], pb[:], ACT.Copy, scale=inv_sum_b[:])
        factor = sb.tile([P, G], F32, name="factor")
        nc.vector.tensor_tensor(factor[:], mb[:].indirect(pages[:]), inv_den[:], ALU.mult)

        num = sb.tile([P, G], F32, name="num")
        prod = []
        for h in range(2):
            dp = product("dp%d" % h, g_mx, vals_got[h], vals_sc[VALS_ROW:P, h * HALF : (h + 1) * HALF])
            prod_h = sb.tile([P, HALF], F32, name="prod%d" % h)
            nc.vector.scalar_tensor_tensor(prod_h[:], dp[:], 256.0, pa[h][:], ALU.mult, ALU.mult)
            prod.append(prod_h)
        for h in range(2):
            nc.vector.tensor_reduce(
                num[:, h * (G // 2) : (h + 1) * (G // 2)], prod[h][:].rearrange("p (g j) -> p g j", j=PAGE), AX.X, ALU.add
            )

        nc.vector.tensor_tensor(mf[:].indirect(pages[:]), num[:], factor[:], ALU.mult)
        neg_md = sb.tile([P, G], F32, name="neg_md")
        neg_total = sb.tile([P, 1], F32, name="neg_total")
        nc.vector.scalar_tensor_tensor(neg_md[:], num[:], -1.0, factor[:], ALU.mult, ALU.mult, accum_out=neg_total[:])
        for h, queue in enumerate((nc.sync, nc.scalar)):
            cols = slice(h * (U // 2), (h + 1) * (U // 2))
            y = sb.tile([P, U // 2], F32, name="y%d" % h)
            nc.vector.scalar_tensor_tensor(y[:], mb[:, cols], neg_total[:], mf[:, cols], ALU.mult, ALU.add)
            queue.dma_start(out=out[:, cols], in_=y[:])
